import numpy as np
import ml_dtypes


def mxq(x, axis, fmt="e4m3"):
    dtype, down = {"e4m3": (ml_dtypes.float8_e4m3fn, 7), "e5m2": (ml_dtypes.float8_e5m2, 14)}[fmt]
    v = np.moveaxis(np.asarray(x, np.float32).astype(ml_dtypes.bfloat16).astype(np.float64), axis, -1)
    blocks = v.reshape(v.shape[:-1] + (-1, 32))
    amax = np.abs(blocks).max(-1, keepdims=True)
    byte = np.maximum(np.where(amax > 0, np.frexp(amax)[1] - 1 + 127, 0) - down, 1)
    scale = np.exp2(byte - 127.0)
    codes = (blocks / scale).astype(np.float32).astype(dtype).astype(np.float64)
    return np.moveaxis((codes * scale).reshape(v.shape), -1, axis)


WIDE = False


def mx_kscale(k):
    if not WIDE:
        return np.ones(k)
    levels = np.array([10, -10, 5, -5, 0])
    if k % 512:
        return np.exp2(np.random.permutation(np.resize(levels, k // 32))).repeat(32)
    a = np.empty((k // 512, 16))
    for p in range(k // 512):
        a[p, :8] = np.random.permutation(np.resize(levels, 8))
        for g in range(8):
            far = levels[np.abs(levels - a[p, g]) >= 10]
            a[p, g + 8] = far[np.random.randint(len(far))]
    return np.exp2(a.ravel()).repeat(32)


def f64(x):
    return np.asarray(x).astype(np.float64)


def striped(idx):
    return np.tile(idx.reshape(-1, 16).T, (8, 1)).astype(np.uint16)


def unstriped(offs):
    return offs[:16].T.reshape(-1).astype(np.int64)


def pack_weight(w):
    k, n = w.shape
    w = f64(np.asarray(w, np.float32).astype(ml_dtypes.bfloat16)).reshape(k // 32, 32, n)
    amax = np.abs(w).max(1)
    byte = np.clip(np.where(amax > 0, np.frexp(amax)[1] - 1 + 127 - 7, 1), 1, 254)
    scaled = (w * np.exp2(127.0 - byte)[:, None, :]).reshape(k, n).astype(np.float32)
    words = np.ascontiguousarray(scaled.reshape(k // 512, 128, 4, n).transpose(0, 1, 3, 2)).astype(ml_dtypes.float8_e4m3fn).view(np.uint8)
    return words, np.ascontiguousarray(byte.astype(np.uint8).reshape(k // 512, 16, n))


def unpack_weight(words, scales):
    g, p, n, _ = words.shape
    vals = np.ascontiguousarray(words).view(ml_dtypes.float8_e4m3fn).astype(np.float64) * np.repeat(np.exp2(scales.astype(np.float64) - 127.0), 8, axis=1)[..., None]
    return vals.transpose(0, 1, 3, 2).reshape(g * 512, n)


E2M1 = np.array([0.0, 0.5, 1.0, 1.5, 2.0, 3.0, 4.0, 6.0, -0.0, -0.5, -1.0, -1.5, -2.0, -3.0, -4.0, -6.0])


def pack_fp4(w):
    k, n = w.shape
    w = f64(np.asarray(w, np.float32).astype(ml_dtypes.bfloat16)).reshape(k // 32, 32, n)
    amax = np.abs(w).max(1)
    mant, ex = np.frexp(amax / 6.0)
    byte = np.clip(np.where(amax > 0, np.where(mant > 0.5, ex, ex - 1) + 127, 1), 1, 254)
    scaled = (w * np.exp2(127.0 - byte)[:, None, :]).reshape(k, n).astype(np.float32)
    c = np.ascontiguousarray(scaled.reshape(k // 512, 128, 4, n).transpose(0, 1, 3, 2)).astype(ml_dtypes.float4_e2m1fn).view(np.uint8) & 0xF
    words = (c[..., 0::2] | (c[..., 1::2] << 4)).reshape(k // 512, 128, 2 * n)
    return np.ascontiguousarray(words), np.ascontiguousarray(byte.astype(np.uint8).reshape(k // 512, 16, n))


def unpack_fp4(words, scales):
    g, _, n = scales.shape
    words = np.ascontiguousarray(words).reshape(g, 128, n, 2)
    nib = np.empty((g, 128, n, 4), np.uint8)
    nib[..., 0::2] = words & 0xF
    nib[..., 1::2] = words >> 4
    vals = E2M1[nib] * np.repeat(np.exp2(scales.astype(np.float64) - 127.0), 8, axis=1)[..., None]
    return vals.transpose(0, 1, 3, 2).reshape(g * 512, n)


def relu(v):
    return np.maximum(v, 0.0)


def sigmoid(v):
    return 1.0 / (1.0 + np.exp(-np.maximum(v, -700.0)))


K, T, S, N, H = 1024, 1024, 512, 256, 512


def setup_inputs():
    n = np.random.standard_normal
    s = mx_kscale(K)[:, None]
    u = mx_kscale(H)
    packed_xT = pack_weight(n((K, T)) * s)
    packed_w1 = pack_fp4(n((K, H)) / np.sqrt(K) / s)
    packed_w2 = pack_fp4(n((H, N)) / np.sqrt(H) / u[:, None])
    return {
        "x_words": packed_xT[0],
        "x_scales": packed_xT[1],
        "w1_words": packed_w1[0],
        "w1_scales": packed_w1[1],
        "thr": (np.random.uniform(0.6, 1.2, (H, S))).astype(np.float32),
        "unit": (np.random.uniform(0.6, 1.4, (H, 1)) * u[:, None]).astype(np.float32),
        "w2_words": packed_w2[0],
        "w2_scales": packed_w2[1],
        "offs": striped(np.random.permutation(T)[:S]),
        "cn1": striped(np.random.permutation(S)),
        "cn2": striped(np.random.permutation(S)),
        "cn3": striped(np.random.permutation(S)),
    }


def reference(x_words, x_scales, w1_words, w1_scales, thr, unit, w2_words, w2_scales, offs, cn1, cn2, cn3):
    xq = unpack_weight(x_words, x_scales)[:, unstriped(offs)]
    y = unpack_fp4(w1_words, w1_scales).T @ xq
    gate = sigmoid(y)
    g1 = gate[:, unstriped(cn1)]
    g2 = gate[:, unstriped(cn2)]
    g3 = gate[:, unstriped(cn3)]
    drv = 0.9 * gate + 0.5 * (g1 + 0.6 * g2 + 0.3 * g3) - f64(thr)
    rate = drv / (np.exp(-1.0 * np.abs(drv)) + 0.4)
    ds = 0.6 * ((-1.0 * gate + 1.0) * relu(rate)) - (0.4 * gate)
    hc = rate[:, unstriped(cn1)]
    hid = f64(unit) * (ds * hc)
    return unpack_fp4(w2_words, w2_scales).T @ mxq(hid, 0, "e4m3")

@@ -1,0 +1,237 @@
+import math
+from contextlib import ExitStack
+
+import concourse.mybir as mybir
+from concourse.masks import make_identity
+
+F32 = mybir.dt.float32
+BF16 = mybir.dt.bfloat16
+I32 = mybir.dt.int32
+U32 = mybir.dt.uint32
+U16 = mybir.dt.uint16
+U8 = mybir.dt.uint8
+FP8X4 = mybir.dt.float8_e4m3fn_x4
+FP4X4 = mybir.dt.float4_e2m1fn_x4
+ALU = mybir.AluOpType
+ACT = mybir.ActivationFunctionType
+
+K, T, S, H, N = 1024, 1024, 512, 512, 256
+P = 128
+PACK = 4
+PASSES = K // (P * PACK)
+FLOPS = 2 * K * H * S + 2 * H * N * S
+
+SHIFT = 8.0 / 15.0
+ROW = 1.25 * 0.75 / 0.9
+HALF = S // 2
+HC = "SSSX"
+N2 = "VVVV"
+ORDER = "A0 A1 B0 A2 R0 B1 A3 W0 R1 B2 H0 W1 R2 B3 H1 W2 R3 H2 W3 H3"
+
+
+def tile_picked_ydmfst_mul_p_kernel(
+    tc, x_words, x_scales, w1_words, w1_scales, thr, unit, w2_words, w2_scales, offs, cn1, cn2, cn3, out
+):
+    nc = tc.nc
+    with ExitStack() as ctx:
+        keep = ctx.enter_context(tc.tile_pool(name="keep", bufs=1))
+        ring = ctx.enter_context(tc.tile_pool(name="ring", bufs=2))
+        near = ctx.enter_context(tc.tile_pool(name="near", bufs=2))
+        psum = ctx.enter_context(tc.psum_pool(name="psum", bufs=1))
+
+        def scale_rows(tile, scales, passes):
+            for q in range(4):
+                nc.sync.dma_start(
+                    out=tile[32 * q : 32 * q + 4, :].bitcast(I32).rearrange("r (o n) -> r o n", o=passes),
+                    in_=scales[:, 4 * q : 4 * q + 4, :].bitcast(I32).rearrange("o r n -> r o n"),
+                )
+
+        xs_raw = keep.tile([P, PASSES * T], U8, align_bytes=64)
+        w1s_raw = keep.tile([P, PASSES * H], U8, align_bytes=64)
+        w2s = keep.tile([P, N], U8, align_bytes=64)
+        nc.vector.memset(xs_raw[:].bitcast(I32), 0)
+        nc.gpsimd.memset(w1s_raw[:].bitcast(I32), 0)
+        nc.gpsimd.memset(w2s[:].bitcast(I32), 0)
+
+        offs_sb = keep.tile([P, S // 16], U16)
+        nc.sync.dma_start(offs_sb[:], offs)
+        w1w_raw = keep.tile([P, PASSES, 2 * H], U8, align_bytes=64)
+        nc.sync.dma_start(out=w1w_raw[:].bitcast(I32), in_=w1_words.bitcast(I32).rearrange("o p n -> p o n"))
+        scale_rows(xs_raw, x_scales, PASSES)
+        xw_raw = [keep.tile([P, T], I32, name=f"xw_raw{o}", align_bytes=64) for o in range(PASSES)]
+        nc.sync.dma_start(out=xw_raw[0][:], in_=x_words[0].rearrange("p n r -> p (n r)").bitcast(I32))
+        scale_rows(w1s_raw, w1_scales, PASSES)
+        nc.sync.dma_start(out=xw_raw[1][:], in_=x_words[1].rearrange("p n r -> p (n r)").bitcast(I32))
+        cn3_sb = keep.tile([P, S // 16], U16)
+        nc.sync.dma_start(cn3_sb[:], cn3)
+        cn1_sb = keep.tile([P, S // 16], U16)
+        nc.sync.dma_start(cn1_sb[:], cn1)
+        cn2_sb = keep.tile([P, S // 16], U16)
+        nc.sync.dma_start(cn2_sb[:], cn2)
+        thr_rows = thr.rearrange("(p t) j -> p t j", t=PACK)
+        thr_sb = [keep.tile([P, S], F32, name=f"thr_sb{t}") for t in range(PACK)]
+        for t in range(PACK):
+            nc.sync.dma_start(out=thr_sb[t][:], in_=thr_rows[:, t, :])
+        unit_sb = keep.tile([P, PACK], F32)
+        nc.sync.dma_start(out=unit_sb[:], in_=unit.rearrange("(p t) o -> p (t o)", t=PACK))
+        w2w = keep.tile([P, 2 * N], U8, align_bytes=64)
+        nc.sync.dma_start(out=w2w[:].bitcast(I32), in_=w2_words[0].bitcast(I32))
+        scale_rows(w2s, w2_scales, 1)
+
+        ident = keep.tile([P, P], F32)
+        make_identity(nc, ident[:])
+        ones = keep.tile([P, P], F32)
+        nc.gpsimd.memset(ones[:], 1.0)
+        shift = keep.tile([P, P], F32)
+        nc.gpsimd.tensor_scalar(shift[:], ones[:], -SHIFT, 0.0, ALU.mult, ALU.add)
+        tanh_bias = keep.tile([P, 1], F32)
+        nc.gpsimd.tensor_scalar(tanh_bias[:], ones[:, 0:1], -0.5 * math.log(2.5), 0.0, ALU.mult, ALU.add)
+        row_scale = keep.tile([P, PACK], F32)
+        nc.gpsimd.tensor_scalar(row_scale[:], unit_sb[:], ROW, 0.0, ALU.mult, ALU.add)
+        row_bias = keep.tile([P, PACK], F32)
+        nc.gpsimd.tensor_scalar(row_bias[:], unit_sb[:], ROW * SHIFT, 0.0, ALU.mult, ALU.add)
+
+        def add_transposed(bank, src, start, stop):
+            for b in range(S // P):
+                cols = slice(b * P, (b + 1) * P)
+                nc.tensor.matmul(
+                    bank[:, cols],
+                    lhsT=src(cols),
+                    rhs=ident[:],
+                    is_transpose=True,
+                    start=start and b == 0,
+                    stop=stop and b == S // P - 1,
+                )
+
+        gate_win = [keep.tile([P, 4 * S], F32, name=f"gate_win{t}") for t in range(PACK)]
+        rate_win = [keep.tile([P, 2 * S], F32, name=f"rate_win{t}") for t in range(PACK)]
+        drive = [psum.tile([P, S], F32, name=f"drive{t}") for t in range(PACK)]
+
+        w1w = [keep.tile([P, PASSES, 2 * P], U8, name=f"w1w{t}", align_bytes=64) for t in range(PACK)]
+        w1s = [keep.tile([P, PASSES, P], U8, name=f"w1s{t}", align_bytes=64) for t in range(PACK)]
+
+        def deal(t):
+            nc.vector.tensor_copy(
+                w1w[t][:].rearrange("p o (m b) -> p o m b", b=2),
+                w1w_raw[:].rearrange("p o (m t b) -> p o t m b", t=PACK, b=2)[:, :, t],
+            )
+            nc.vector.tensor_copy(
+                w1s[t][:], w1s_raw[:].rearrange("p (o m t) -> p o t m", o=PASSES, t=PACK)[:, :, t]
+            )
+
+        xw = [keep.tile([P, S], U32, name=f"xw{o}", align_bytes=64) for o in range(PASSES)]
+        xs = [keep.tile([P, S], U8, name=f"xs{o}", align_bytes=64) for o in range(PASSES)]
+        for o in range(PASSES):
+            nc.vector.tensor_copy(xs[o][:], xs_raw[:, o * T : (o + 1) * T].indirect(offs_sb[:]))
+        nc.vector.tensor_copy(xw[0][:], xw_raw[0][:].bitcast(U32).indirect(offs_sb[:]))
+        deal(0)
+        nc.vector.tensor_copy(xw[1][:], xw_raw[1][:].bitcast(U32).indirect(offs_sb[:]))
+        for t in range(1, PACK):
+            deal(t)
+
+        closed = [keep.tile([P, S], F32, name=f"closed{t}") for t in range(PACK)]
+        filled = [keep.tile([P, S], F32, name=f"filled{t}") for t in range(PACK)]
+        hid = keep.tile([P, PACK, S], BF16, align_bytes=64)
+        bound = {}
+        shifted = {}
+
+        def drive_stage(t):
+            y = psum.tile([P, S], F32, name="y", tag=f"bank{t % 2}")
+            for o in range(PASSES):
+                nc.tensor.matmul_mx(
+                    y[:],
+                    lhsT=w1w[t][:, o, :].bitcast(FP4X4),
+                    lhsT_scale=w1s[t][:, o, :],
+                    rhs=xw[o][:].bitcast(FP8X4),
+                    rhs_scale=xs[o][:],
+                    start=o == 0,
+                    stop=o == PASSES - 1,
+                )
+            win = gate_win[t]
+            nc.scalar.activation(win[:, :S], y[:], ACT.Tanh, scale=-0.5)
+            nc.vector.tensor_scalar(closed[t][:], win[:, :S], 0.45, 0.45, ALU.mult, ALU.add)
+            add_transposed(drive[t], lambda cols: closed[t][:, cols], True, False)
+            n3 = near.tile([P, S], F32, name="n3")
+            nc.scalar.activation(n3[:], win[:].indirect(cn3_sb[:]), ACT.Copy, scale=0.075)
+            n1 = near.tile([P, S], F32, name="n1")
+            nc.vector.tensor_scalar(n1[:], win[:].indirect(cn1_sb[:]), 0.25, -1.375, ALU.mult, ALU.add)
+            n2 = near.tile([P, S], F32, name="n2")
+            if N2[t] == "V":
+                nc.vector.tensor_scalar(n2[:], win[:].indirect(cn2_sb[:]), 0.15, 0.0, ALU.mult, ALU.add)
+            else:
+                nc.scalar.activation(n2[:], win[:].indirect(cn2_sb[:]), ACT.Copy, scale=0.15)
+            add_transposed(drive[t], lambda cols: n3[:, cols], False, False)
+            add_transposed(drive[t], lambda cols: n1[:, cols], False, False)
+            add_transposed(drive[t], lambda cols: thr_sb[t][:, cols], False, False)
+            add_transposed(drive[t], lambda cols: n2[:, cols], False, True)
+
+        def bound_stage(t):
+            size = ring.tile([P, S], F32, name="size")
+            nc.scalar.activation(size[:], drive[t][:], ACT.Abs)
+            bound[t] = ring.tile([P, S], F32, name="bound")
+            nc.scalar.activation(bound[t][:], size[:], ACT.Tanh, bias=tanh_bias[:], scale=0.5)
+
+        def rate_stage(t):
+            rate_t = ring.tile([P, S], F32, name="rate_t")
+            nc.vector.scalar_tensor_tensor(rate_t[:], bound[t][:], 1.0, drive[t][:], ALU.add, ALU.mult)
+            shifted[t] = psum.tile([P, S], F32, name="shifted", tag=f"bank{(t + 2) % 4}")
+            add_transposed(shifted[t], lambda cols: shift[:], True, False)
+            add_transposed(shifted[t], lambda cols: rate_t[:, cols], False, True)
+
+        def window_stage(t):
+            nc.scalar.activation(
+                rate_win[t][:, :S], shifted[t][:], ACT.Identity, bias=row_bias[:, t : t + 1], scale=row_scale[:, t : t + 1]
+            )
+            nc.vector.scalar_tensor_tensor(filled[t][:], shifted[t][:], -SHIFT, closed[t][:], ALU.min, ALU.mult)
+
+        def hidden_stage(t):
+            win = rate_win[t]
+            if HC[t] == "X":
+                for a in range(2):
+                    cols = slice(a * HALF, (a + 1) * HALF)
+                    part = ring.tile([P, HALF], F32, name="part")
+                    picked = win[:].indirect(cn1_sb[:, a * HALF // 16 : (a + 1) * HALF // 16])
+                    if a == 0:
+                        nc.scalar.activation(part[:], picked, ACT.Copy)
+                    else:
+                        nc.vector.tensor_copy(part[:], picked)
+                    nc.vector.scalar_tensor_tensor(hid[:, t, cols], filled[t][:, cols], 0.48, part[:], ALU.add, ALU.mult)
+            else:
+                hc = ring.tile([P, S], F32, name="hc")
+                if HC[t] == "S":
+                    nc.scalar.activation(hc[:], win[:].indirect(cn1_sb[:]), ACT.Copy)
+                else:
+                    nc.vector.tensor_copy(hc[:], win[:].indirect(cn1_sb[:]))
+                nc.vector.scalar_tensor_tensor(hid[:, t, :], filled[t][:], 0.48, hc[:], ALU.add, ALU.mult)
+
+        stages = {"A": drive_stage, "B": bound_stage, "R": rate_stage, "W": window_stage, "H": hidden_stage}
+        for word in ORDER.split():
+            stages[word[0]](int(word[1]))
+
+        for a in range(2):
+            cols = slice(a * HALF, (a + 1) * HALF)
+            woven = ring.tile([P, HALF, PACK], BF16, name="woven", align_bytes=64)
+            nc.vector.tensor_copy(
+                woven[:].rearrange("p (c i) t -> p c t i", i=4),
+                hid[:, :, cols].rearrange("p t (c i) -> p c t i", i=4),
+            )
+            codes = ring.tile([P, HALF], U32, name="codes", align_bytes=64)
+            scales = ring.tile([P, HALF], U8, name="scales", align_bytes=64)
+            nc.vector.quantize_mx(codes[:].bitcast(FP8X4), scales[:], woven[:].rearrange("p j t -> p (j t)"))
+            for b in range(N // P):
+                acc = psum.tile([P, HALF], F32, name="acc", tag=f"drive{2 * a + b}")
+                nc.tensor.matmul_mx(
+                    acc[:],
+                    lhsT=w2w[:, 2 * P * b : 2 * P * (b + 1)].bitcast(FP4X4),
+                    lhsT_scale=w2s[:, P * b : P * (b + 1)],
+                    rhs=codes[:].bitcast(FP8X4),
+                    rhs_scale=scales[:],
+                    start=True,
+                    stop=True,
+                )
+                result = keep.tile([P, HALF], F32, name=f"result{a}{b}")
+                if a == 1 and b == 1:
+                    nc.vector.tensor_copy(result[:], acc[:])
+                else:
+                    nc.scalar.copy(result[:], acc[:])
+                nc.sync.dma_start(out=out[b * P : (b + 1) * P, cols], in_=result[:])

@@ -25,8 +25,9 @@ SHIFT = 8.0 / 15.0
 ROW = 1.25 * 0.75 / 0.9
 HALF = S // 2
 HC = "SSSX"
-N2 = "VVVV"
-ORDER = "A0 A1 B0 A2 R0 B1 A3 W0 R1 B2 H0 W1 R2 B3 H1 W2 R3 H2 W3 H3"
+N2 = "SVVV"
+MODE = "NPPP"
+ORDER = "A0 A1 B0 R0 A2 B1 R1 W0 A3 B2 R2 W1 B3 R3 H0 W2 H1 W3 H2 H3"
 
 
 def tile_picked_ydmfst_mul_p_kernel(
@@ -39,57 +40,65 @@ def tile_picked_ydmfst_mul_p_kernel(
         near = ctx.enter_context(tc.tile_pool(name="near", bufs=2))
         psum = ctx.enter_context(tc.psum_pool(name="psum", bufs=1))
 
-        def scale_rows(tile, scales, passes):
-            for q in range(4):
-                nc.sync.dma_start(
-                    out=tile[32 * q : 32 * q + 4, :].bitcast(I32).rearrange("r (o n) -> r o n", o=passes),
-                    in_=scales[:, 4 * q : 4 * q + 4, :].bitcast(I32).rearrange("o r n -> r o n"),
-                )
-
-        xs_raw = keep.tile([P, PASSES * T], U8, align_bytes=64)
+        xs_raw = keep.tile([P, T], U8, align_bytes=64)
+        xs_second = keep.tile([P, S], U8, align_bytes=64)
         w1s_raw = keep.tile([P, PASSES * H], U8, align_bytes=64)
         w2s = keep.tile([P, N], U8, align_bytes=64)
-        nc.vector.memset(xs_raw[:].bitcast(I32), 0)
+        nc.gpsimd.memset(xs_raw[:].bitcast(I32), 0)
         nc.gpsimd.memset(w1s_raw[:].bitcast(I32), 0)
-        nc.gpsimd.memset(w2s[:].bitcast(I32), 0)
+        nc.vector.memset(xs_second[:].bitcast(I32), 0)
+        nc.vector.memset(w2s[:].bitcast(I32), 0)
 
         offs_sb = keep.tile([P, S // 16], U16)
         nc.sync.dma_start(offs_sb[:], offs)
-        w1w_raw = keep.tile([P, PASSES, 2 * H], U8, align_bytes=64)
-        nc.sync.dma_start(out=w1w_raw[:].bitcast(I32), in_=w1_words.bitcast(I32).rearrange("o p n -> p o n"))
-        scale_rows(xs_raw, x_scales, PASSES)
+        for q in range(4):
+            nc.sync.dma_start(
+                out=xs_raw[32 * q : 32 * q + 8, :].bitcast(I32), in_=x_scales[:, 4 * q : 4 * q + 4, :].bitcast(I32)
+            )
         xw_raw = [keep.tile([P, T], I32, name=f"xw_raw{o}", align_bytes=64) for o in range(PASSES)]
         nc.sync.dma_start(out=xw_raw[0][:], in_=x_words[0].rearrange("p n r -> p (n r)").bitcast(I32))
-        scale_rows(w1s_raw, w1_scales, PASSES)
+        for q in range(4):
+            queue = nc.gpsimd if q < 2 else nc.sync
+            queue.dma_start(
+                out=w1s_raw[32 * q : 32 * q + 4, :].bitcast(I32).rearrange("r (o n) -> r o n", o=PASSES),
+                in_=w1_scales[:, 4 * q : 4 * q + 4, :].bitcast(I32).rearrange("o r n -> r o n"),
+            )
+        w1w_raw = keep.tile([P, PASSES, 2 * H], U8, align_bytes=64)
+        nc.sync.dma_start(out=w1w_raw[:].bitcast(I32), in_=w1_words.bitcast(I32).rearrange("o p n -> p o n"))
         nc.sync.dma_start(out=xw_raw[1][:], in_=x_words[1].rearrange("p n r -> p (n r)").bitcast(I32))
+        thr_rows = thr.rearrange("(p t) j -> p t j", t=PACK)
+        thr_sb = [keep.tile([P, S], F32, name=f"thr_sb{t}") for t in range(PACK)]
         cn3_sb = keep.tile([P, S // 16], U16)
         nc.sync.dma_start(cn3_sb[:], cn3)
         cn1_sb = keep.tile([P, S // 16], U16)
         nc.sync.dma_start(cn1_sb[:], cn1)
         cn2_sb = keep.tile([P, S // 16], U16)
         nc.sync.dma_start(cn2_sb[:], cn2)
-        thr_rows = thr.rearrange("(p t) j -> p t j", t=PACK)
-        thr_sb = [keep.tile([P, S], F32, name=f"thr_sb{t}") for t in range(PACK)]
         for t in range(PACK):
             nc.sync.dma_start(out=thr_sb[t][:], in_=thr_rows[:, t, :])
         unit_sb = keep.tile([P, PACK], F32)
         nc.sync.dma_start(out=unit_sb[:], in_=unit.rearrange("(p t) o -> p (t o)", t=PACK))
         w2w = keep.tile([P, 2 * N], U8, align_bytes=64)
         nc.sync.dma_start(out=w2w[:].bitcast(I32), in_=w2_words[0].bitcast(I32))
-        scale_rows(w2s, w2_scales, 1)
+        for q in range(4):
+            nc.sync.dma_start(
+                out=w2s[32 * q : 32 * q + 4, :].bitcast(I32), in_=w2_scales[0, 4 * q : 4 * q + 4, :].bitcast(I32)
+            )
 
         ident = keep.tile([P, P], F32)
         make_identity(nc, ident[:])
         ones = keep.tile([P, P], F32)
-        nc.gpsimd.memset(ones[:], 1.0)
+        nc.vector.memset(ones[:], 1.0)
         shift = keep.tile([P, P], F32)
-        nc.gpsimd.tensor_scalar(shift[:], ones[:], -SHIFT, 0.0, ALU.mult, ALU.add)
+        nc.vector.tensor_scalar(shift[:], ones[:], -SHIFT, 0.0, ALU.mult, ALU.add)
         tanh_bias = keep.tile([P, 1], F32)
-        nc.gpsimd.tensor_scalar(tanh_bias[:], ones[:, 0:1], -0.5 * math.log(2.5), 0.0, ALU.mult, ALU.add)
+        nc.vector.tensor_scalar(tanh_bias[:], ones[:, 0:1], -0.5 * math.log(2.5), 0.0, ALU.mult, ALU.add)
         row_scale = keep.tile([P, PACK], F32)
-        nc.gpsimd.tensor_scalar(row_scale[:], unit_sb[:], ROW, 0.0, ALU.mult, ALU.add)
+        nc.vector.tensor_scalar(row_scale[:], unit_sb[:], ROW, 0.0, ALU.mult, ALU.add)
+        row_plain = keep.tile([P, PACK], F32)
+        nc.vector.tensor_scalar(row_plain[:], unit_sb[:], ROW * 0.45, 0.0, ALU.mult, ALU.add)
         row_bias = keep.tile([P, PACK], F32)
-        nc.gpsimd.tensor_scalar(row_bias[:], unit_sb[:], ROW * SHIFT, 0.0, ALU.mult, ALU.add)
+        nc.vector.tensor_scalar(row_bias[:], unit_sb[:], ROW * SHIFT, 0.0, ALU.mult, ALU.add)
 
         def add_transposed(bank, src, start, stop):
             for b in range(S // P):
@@ -105,29 +114,34 @@ def tile_picked_ydmfst_mul_p_kernel(
 
         gate_win = [keep.tile([P, 4 * S], F32, name=f"gate_win{t}") for t in range(PACK)]
         rate_win = [keep.tile([P, 2 * S], F32, name=f"rate_win{t}") for t in range(PACK)]
-        drive = [psum.tile([P, S], F32, name=f"drive{t}") for t in range(PACK)]
+        drive = {}
 
-        w1w = [keep.tile([P, PASSES, 2 * P], U8, name=f"w1w{t}", align_bytes=64) for t in range(PACK)]
-        w1s = [keep.tile([P, PASSES, P], U8, name=f"w1s{t}", align_bytes=64) for t in range(PACK)]
-
-        def deal(t):
+        def deal(first, count, tag):
+            dealt = keep.tile([P, count * PASSES * 3 * P], U8, name="dealt", tag=tag, align_bytes=64)
+            words = dealt[:, : count * PASSES * 2 * P].rearrange("p (t o c) -> p t o c", t=count, o=PASSES)
+            scales = dealt[:, count * PASSES * 2 * P :].rearrange("p (t o m) -> p t o m", t=count, o=PASSES)
             nc.vector.tensor_copy(
-                w1w[t][:].rearrange("p o (m b) -> p o m b", b=2),
-                w1w_raw[:].rearrange("p o (m t b) -> p o t m b", t=PACK, b=2)[:, :, t],
+                words.rearrange("p t o (m b) -> p o t m b", b=2),
+                w1w_raw[:].rearrange("p o (m t b) -> p o t m b", t=PACK, b=2)[:, :, first : first + count],
             )
             nc.vector.tensor_copy(
-                w1s[t][:], w1s_raw[:].rearrange("p (o m t) -> p o t m", o=PASSES, t=PACK)[:, :, t]
+                scales.rearrange("p t o m -> p o t m"),
+                w1s_raw[:].rearrange("p (o m t) -> p o t m", o=PASSES, t=PACK)[:, :, first : first + count],
             )
+            return [(words[:, t], scales[:, t]) for t in range(count)]
 
         xw = [keep.tile([P, S], U32, name=f"xw{o}", align_bytes=64) for o in range(PASSES)]
-        xs = [keep.tile([P, S], U8, name=f"xs{o}", align_bytes=64) for o in range(PASSES)]
-        for o in range(PASSES):
-            nc.vector.tensor_copy(xs[o][:], xs_raw[:, o * T : (o + 1) * T].indirect(offs_sb[:]))
+        xs_both = keep.tile([P, S], U8, align_bytes=64)
+        nc.vector.tensor_copy(xs_both[:], xs_raw[:].indirect(offs_sb[:]))
+        for q in range(4):
+            nc.scalar.dma_start(
+                out=xs_second[32 * q : 32 * q + 4, :].bitcast(I32), in_=xs_both[32 * q + 4 : 32 * q + 8, :].bitcast(I32)
+            )
+        xs = [xs_both, xs_second]
         nc.vector.tensor_copy(xw[0][:], xw_raw[0][:].bitcast(U32).indirect(offs_sb[:]))
-        deal(0)
+        w1 = deal(0, 1, "dealt_first")
         nc.vector.tensor_copy(xw[1][:], xw_raw[1][:].bitcast(U32).indirect(offs_sb[:]))
-        for t in range(1, PACK):
-            deal(t)
+        w1 = w1 + deal(1, PACK - 1, "xw_raw1")
 
         closed = [keep.tile([P, S], F32, name=f"closed{t}") for t in range(PACK)]
         filled = [keep.tile([P, S], F32, name=f"filled{t}") for t in range(PACK)]
@@ -140,8 +154,8 @@ def tile_picked_ydmfst_mul_p_kernel(
             for o in range(PASSES):
                 nc.tensor.matmul_mx(
                     y[:],
-                    lhsT=w1w[t][:, o, :].bitcast(FP4X4),
-                    lhsT_scale=w1s[t][:, o, :],
+                    lhsT=w1[t][0][:, o, :].bitcast(FP4X4),
+                    lhsT_scale=w1[t][1][:, o, :],
                     rhs=xw[o][:].bitcast(FP8X4),
                     rhs_scale=xs[o][:],
                     start=o == 0,
@@ -149,21 +163,36 @@ def tile_picked_ydmfst_mul_p_kernel(
                 )
             win = gate_win[t]
             nc.scalar.activation(win[:, :S], y[:], ACT.Tanh, scale=-0.5)
-            nc.vector.tensor_scalar(closed[t][:], win[:, :S], 0.45, 0.45, ALU.mult, ALU.add)
-            add_transposed(drive[t], lambda cols: closed[t][:, cols], True, False)
+            plain = MODE[t] == "N"
+            if plain:
+                own = ring.tile([P, S], F32, name="partial")
+                nc.vector.scalar_tensor_tensor(own[:], win[:, :S], 0.45, thr_sb[t][:], ALU.mult, ALU.add)
+            else:
+                drive[t] = psum.tile([P, S], F32, name=f"drive{t}")
+                add_transposed(drive[t], lambda cols: thr_sb[t][:, cols], True, False)
+                nc.vector.tensor_scalar(closed[t][:], win[:, :S], 0.45, 0.45, ALU.mult, ALU.add)
+                add_transposed(drive[t], lambda cols: closed[t][:, cols], False, False)
             n3 = near.tile([P, S], F32, name="n3")
             nc.scalar.activation(n3[:], win[:].indirect(cn3_sb[:]), ACT.Copy, scale=0.075)
             n1 = near.tile([P, S], F32, name="n1")
-            nc.vector.tensor_scalar(n1[:], win[:].indirect(cn1_sb[:]), 0.25, -1.375, ALU.mult, ALU.add)
+            nc.vector.tensor_scalar(
+                n1[:], win[:].indirect(cn1_sb[:]), 0.25, -0.925 if plain else -1.375, ALU.mult, ALU.add
+            )
             n2 = near.tile([P, S], F32, name="n2")
             if N2[t] == "V":
                 nc.vector.tensor_scalar(n2[:], win[:].indirect(cn2_sb[:]), 0.15, 0.0, ALU.mult, ALU.add)
             else:
                 nc.scalar.activation(n2[:], win[:].indirect(cn2_sb[:]), ACT.Copy, scale=0.15)
-            add_transposed(drive[t], lambda cols: n3[:, cols], False, False)
-            add_transposed(drive[t], lambda cols: n1[:, cols], False, False)
-            add_transposed(drive[t], lambda cols: thr_sb[t][:, cols], False, False)
-            add_transposed(drive[t], lambda cols: n2[:, cols], False, True)
+            if plain:
+                two = ring.tile([P, S], F32, name="partial")
+                nc.vector.tensor_tensor(two[:], own[:], n3[:], ALU.add)
+                nc.vector.tensor_tensor(own[:], two[:], n1[:], ALU.add)
+                drive[t] = keep.tile([P, S], F32, name=f"drive_sb{t}")
+                nc.vector.tensor_tensor(drive[t][:], own[:], n2[:], ALU.add)
+            else:
+                add_transposed(drive[t], lambda cols: n3[:, cols], False, False)
+                add_transposed(drive[t], lambda cols: n1[:, cols], False, False)
+                add_transposed(drive[t], lambda cols: n2[:, cols], False, True)
 
         def bound_stage(t):
             size = ring.tile([P, S], F32, name="size")
@@ -172,13 +201,24 @@ def tile_picked_ydmfst_mul_p_kernel(
             nc.scalar.activation(bound[t][:], size[:], ACT.Tanh, bias=tanh_bias[:], scale=0.5)
 
         def rate_stage(t):
+            if MODE[t] == "N":
+                nc.vector.scalar_tensor_tensor(rate_win[t][:, :S], bound[t][:], 1.0, drive[t][:], ALU.add, ALU.mult)
+                return
             rate_t = ring.tile([P, S], F32, name="rate_t")
             nc.vector.scalar_tensor_tensor(rate_t[:], bound[t][:], 1.0, drive[t][:], ALU.add, ALU.mult)
-            shifted[t] = psum.tile([P, S], F32, name="shifted", tag=f"bank{(t + 2) % 4}")
+            shifted[t] = psum.tile([P, S], F32, name="shifted", tag=f"shifted{t}")
             add_transposed(shifted[t], lambda cols: shift[:], True, False)
             add_transposed(shifted[t], lambda cols: rate_t[:, cols], False, True)
 
         def window_stage(t):
+            if MODE[t] == "N":
+                low = ring.tile([P, S], F32, name="partial")
+                nc.vector.tensor_scalar(low[:], rate_win[t][:, :S], 0.0, -SHIFT, ALU.min, ALU.add)
+                nc.vector.scalar_tensor_tensor(closed[t][:], gate_win[t][:, :S], 1.0, low[:], ALU.add, ALU.mult)
+                nc.vector.tensor_scalar(
+                    filled[t][:], closed[t][:], 0.48 / 0.45, row_plain[:, t : t + 1], ALU.add, ALU.mult
+                )
+                return
             nc.scalar.activation(
                 rate_win[t][:, :S], shifted[t][:], ACT.Identity, bias=row_bias[:, t : t + 1], scale=row_scale[:, t : t + 1]
             )
@@ -195,14 +235,14 @@ def tile_picked_ydmfst_mul_p_kernel(
                         nc.scalar.activation(part[:], picked, ACT.Copy)
                     else:
                         nc.vector.tensor_copy(part[:], picked)
-                    nc.vector.scalar_tensor_tensor(hid[:, t, cols], filled[t][:, cols], 0.48, part[:], ALU.add, ALU.mult)
+                    nc.vector.scalar_tensor_tensor(hid[:, t, cols], filled[t][:, cols], 0.0 if MODE[t] == "N" else 0.48, part[:], ALU.add, ALU.mult)
             else:
                 hc = ring.tile([P, S], F32, name="hc")
                 if HC[t] == "S":
                     nc.scalar.activation(hc[:], win[:].indirect(cn1_sb[:]), ACT.Copy)
                 else:
                     nc.vector.tensor_copy(hc[:], win[:].indirect(cn1_sb[:]))
-                nc.vector.scalar_tensor_tensor(hid[:, t, :], filled[t][:], 0.48, hc[:], ALU.add, ALU.mult)
+                nc.vector.scalar_tensor_tensor(hid[:, t, :], filled[t][:], 0.0 if MODE[t] == "N" else 0.48, hc[:], ALU.add, ALU.mult)
 
         stages = {"A": drive_stage, "B": bound_stage, "R": rate_stage, "W": window_stage, "H": hidden_stage}
         for word in ORDER.split():
@@ -219,7 +259,7 @@ def tile_picked_ydmfst_mul_p_kernel(
             scales = ring.tile([P, HALF], U8, name="scales", align_bytes=64)
             nc.vector.quantize_mx(codes[:].bitcast(FP8X4), scales[:], woven[:].rearrange("p j t -> p (j t)"))
             for b in range(N // P):
-                acc = psum.tile([P, HALF], F32, name="acc", tag=f"drive{2 * a + b}")
+                acc = psum.tile([P, HALF], F32, name="acc", tag=("bank0", "bank1", "drive1", "drive2")[2 * a + b])
                 nc.tensor.matmul_mx(
                     acc[:],
                     lhsT=w2w[:, 2 * P * b : 2 * P * (b + 1)].bitcast(FP4X4),

@@ -25,9 +25,9 @@ SHIFT = 8.0 / 15.0
 ROW = 1.25 * 0.75 / 0.9
 HALF = S // 2
 HC = "SSSX"
-N2 = "SVVV"
-MODE = "NPPP"
-ORDER = "A0 A1 B0 R0 A2 B1 R1 W0 A3 B2 R2 W1 B3 R3 H0 W2 H1 W3 H2 H3"
+N2 = "VSVS"
+MODE = "NPPN"
+ORDER = "A0 A1 B0 A2 B1 R0 A3 B2 R1 W0 B3 R2 W1 R3 W2 W3 H0 H1 H2 H3"
 
 
 def tile_picked_ydmfst_mul_p_kernel(
@@ -38,6 +38,7 @@ def tile_picked_ydmfst_mul_p_kernel(
         keep = ctx.enter_context(tc.tile_pool(name="keep", bufs=1))
         ring = ctx.enter_context(tc.tile_pool(name="ring", bufs=2))
         near = ctx.enter_context(tc.tile_pool(name="near", bufs=2))
+        part4 = ctx.enter_context(tc.tile_pool(name="part4", bufs=4))
         psum = ctx.enter_context(tc.psum_pool(name="psum", bufs=1))
 
         xs_raw = keep.tile([P, T], U8, align_bytes=64)
@@ -46,6 +47,8 @@ def tile_picked_ydmfst_mul_p_kernel(
         w2s = keep.tile([P, N], U8, align_bytes=64)
         nc.gpsimd.memset(xs_raw[:].bitcast(I32), 0)
         nc.gpsimd.memset(w1s_raw[:].bitcast(I32), 0)
+        ident = keep.tile([P, P], F32)
+        make_identity(nc, ident[:])
         nc.vector.memset(xs_second[:].bitcast(I32), 0)
         nc.vector.memset(w2s[:].bitcast(I32), 0)
 
@@ -56,16 +59,15 @@ def tile_picked_ydmfst_mul_p_kernel(
                 out=xs_raw[32 * q : 32 * q + 8, :].bitcast(I32), in_=x_scales[:, 4 * q : 4 * q + 4, :].bitcast(I32)
             )
         xw_raw = [keep.tile([P, T], I32, name=f"xw_raw{o}", align_bytes=64) for o in range(PASSES)]
-        nc.sync.dma_start(out=xw_raw[0][:], in_=x_words[0].rearrange("p n r -> p (n r)").bitcast(I32))
+        nc.sync.dma_start(out=xw_raw[1][:], in_=x_words[1].rearrange("p n r -> p (n r)").bitcast(I32))
         for q in range(4):
-            queue = nc.gpsimd if q < 2 else nc.sync
-            queue.dma_start(
+            nc.sync.dma_start(
                 out=w1s_raw[32 * q : 32 * q + 4, :].bitcast(I32).rearrange("r (o n) -> r o n", o=PASSES),
                 in_=w1_scales[:, 4 * q : 4 * q + 4, :].bitcast(I32).rearrange("o r n -> r o n"),
             )
         w1w_raw = keep.tile([P, PASSES, 2 * H], U8, align_bytes=64)
         nc.sync.dma_start(out=w1w_raw[:].bitcast(I32), in_=w1_words.bitcast(I32).rearrange("o p n -> p o n"))
-        nc.sync.dma_start(out=xw_raw[1][:], in_=x_words[1].rearrange("p n r -> p (n r)").bitcast(I32))
+        nc.sync.dma_start(out=xw_raw[0][:], in_=x_words[0].rearrange("p n r -> p (n r)").bitcast(I32))
         thr_rows = thr.rearrange("(p t) j -> p t j", t=PACK)
         thr_sb = [keep.tile([P, S], F32, name=f"thr_sb{t}") for t in range(PACK)]
         cn3_sb = keep.tile([P, S // 16], U16)
@@ -74,6 +76,12 @@ def tile_picked_ydmfst_mul_p_kernel(
         nc.sync.dma_start(cn1_sb[:], cn1)
         cn2_sb = keep.tile([P, S // 16], U16)
         nc.sync.dma_start(cn2_sb[:], cn2)
+        xs_both = keep.tile([P, S], U8, align_bytes=64)
+        nc.vector.tensor_copy(xs_both[:], xs_raw[:].indirect(offs_sb[:]))
+        for q in range(4):
+            nc.sync.dma_start(
+                out=xs_second[32 * q : 32 * q + 4, :].bitcast(I32), in_=xs_both[32 * q + 4 : 32 * q + 8, :].bitcast(I32)
+            )
         for t in range(PACK):
             nc.sync.dma_start(out=thr_sb[t][:], in_=thr_rows[:, t, :])
         unit_sb = keep.tile([P, PACK], F32)
@@ -85,8 +93,6 @@ def tile_picked_ydmfst_mul_p_kernel(
                 out=w2s[32 * q : 32 * q + 4, :].bitcast(I32), in_=w2_scales[0, 4 * q : 4 * q + 4, :].bitcast(I32)
             )
 
-        ident = keep.tile([P, P], F32)
-        make_identity(nc, ident[:])
         ones = keep.tile([P, P], F32)
         nc.vector.memset(ones[:], 1.0)
         shift = keep.tile([P, P], F32)
@@ -131,17 +137,11 @@ def tile_picked_ydmfst_mul_p_kernel(
             return [(words[:, t], scales[:, t]) for t in range(count)]
 
         xw = [keep.tile([P, S], U32, name=f"xw{o}", align_bytes=64) for o in range(PASSES)]
-        xs_both = keep.tile([P, S], U8, align_bytes=64)
-        nc.vector.tensor_copy(xs_both[:], xs_raw[:].indirect(offs_sb[:]))
-        for q in range(4):
-            nc.scalar.dma_start(
-                out=xs_second[32 * q : 32 * q + 4, :].bitcast(I32), in_=xs_both[32 * q + 4 : 32 * q + 8, :].bitcast(I32)
-            )
         xs = [xs_both, xs_second]
-        nc.vector.tensor_copy(xw[0][:], xw_raw[0][:].bitcast(U32).indirect(offs_sb[:]))
-        w1 = deal(0, 1, "dealt_first")
         nc.vector.tensor_copy(xw[1][:], xw_raw[1][:].bitcast(U32).indirect(offs_sb[:]))
-        w1 = w1 + deal(1, PACK - 1, "xw_raw1")
+        w1 = deal(0, 1, "dealt_first")
+        nc.vector.tensor_copy(xw[0][:], xw_raw[0][:].bitcast(U32).indirect(offs_sb[:]))
+        w1 = w1 + deal(1, PACK - 1, "xw_raw0")
 
         closed = [keep.tile([P, S], F32, name=f"closed{t}") for t in range(PACK)]
         filled = [keep.tile([P, S], F32, name=f"filled{t}") for t in range(PACK)]
@@ -151,21 +151,21 @@ def tile_picked_ydmfst_mul_p_kernel(
 
         def drive_stage(t):
             y = psum.tile([P, S], F32, name="y", tag=f"bank{t % 2}")
-            for o in range(PASSES):
+            for o in reversed(range(PASSES)):
                 nc.tensor.matmul_mx(
                     y[:],
                     lhsT=w1[t][0][:, o, :].bitcast(FP4X4),
                     lhsT_scale=w1[t][1][:, o, :],
                     rhs=xw[o][:].bitcast(FP8X4),
                     rhs_scale=xs[o][:],
-                    start=o == 0,
-                    stop=o == PASSES - 1,
+                    start=o == PASSES - 1,
+                    stop=o == 0,
                 )
             win = gate_win[t]
             nc.scalar.activation(win[:, :S], y[:], ACT.Tanh, scale=-0.5)
             plain = MODE[t] == "N"
             if plain:
-                own = ring.tile([P, S], F32, name="partial")
+                own = part4.tile([P, S], F32, name="partial")
                 nc.vector.scalar_tensor_tensor(own[:], win[:, :S], 0.45, thr_sb[t][:], ALU.mult, ALU.add)
             else:
                 drive[t] = psum.tile([P, S], F32, name=f"drive{t}")
@@ -184,7 +184,7 @@ def tile_picked_ydmfst_mul_p_kernel(
             else:
                 nc.scalar.activation(n2[:], win[:].indirect(cn2_sb[:]), ACT.Copy, scale=0.15)
             if plain:
-                two = ring.tile([P, S], F32, name="partial")
+                two = part4.tile([P, S], F32, name="partial")
                 nc.vector.tensor_tensor(two[:], own[:], n3[:], ALU.add)
                 nc.vector.tensor_tensor(own[:], two[:], n1[:], ALU.add)
                 drive[t] = keep.tile([P, S], F32, name=f"drive_sb{t}")
@@ -212,7 +212,7 @@ def tile_picked_ydmfst_mul_p_kernel(
 
         def window_stage(t):
             if MODE[t] == "N":
-                low = ring.tile([P, S], F32, name="partial")
+                low = part4.tile([P, S], F32, name="partial")
                 nc.vector.tensor_scalar(low[:], rate_win[t][:, :S], 0.0, -SHIFT, ALU.min, ALU.add)
                 nc.vector.scalar_tensor_tensor(closed[t][:], gate_win[t][:, :S], 1.0, low[:], ALU.add, ALU.mult)
                 nc.vector.tensor_scalar(

import math
from contextlib import ExitStack

import concourse.mybir as mybir
from concourse.masks import make_identity

F32 = mybir.dt.float32
BF16 = mybir.dt.bfloat16
I32 = mybir.dt.int32
U32 = mybir.dt.uint32
U16 = mybir.dt.uint16
U8 = mybir.dt.uint8
FP8X4 = mybir.dt.float8_e4m3fn_x4
FP4X4 = mybir.dt.float4_e2m1fn_x4
ALU = mybir.AluOpType
ACT = mybir.ActivationFunctionType

K, T, S, H, N = 1024, 1024, 512, 512, 256
P = 128
PACK = 4
PASSES = K // (P * PACK)
FLOPS = 2 * K * H * S + 2 * H * N * S

SHIFT = 8.0 / 15.0
ROW = 1.25 * 0.75 / 0.9
HALF = S // 2
HC = "SSSX"
N2 = "VSVS"
MODE = "NPPN"
ORDER = "A0 A1 B0 A2 B1 R0 A3 B2 R1 W0 B3 R2 W1 R3 W2 W3 H0 H1 H2 H3"


def tile_picked_ydmfst_mul_p_kernel(
    tc, x_words, x_scales, w1_words, w1_scales, thr, unit, w2_words, w2_scales, offs, cn1, cn2, cn3, out
):
    nc = tc.nc
    with ExitStack() as ctx:
        keep = ctx.enter_context(tc.tile_pool(name="keep", bufs=1))
        ring = ctx.enter_context(tc.tile_pool(name="ring", bufs=2))
        near = ctx.enter_context(tc.tile_pool(name="near", bufs=2))
        part4 = ctx.enter_context(tc.tile_pool(name="part4", bufs=4))
        psum = ctx.enter_context(tc.psum_pool(name="psum", bufs=1))

        xs_raw = keep.tile([P, T], U8, align_bytes=64)
        xs_second = keep.tile([P, S], U8, align_bytes=64)
        w1s_raw = keep.tile([P, PASSES * H], U8, align_bytes=64)
        w2s = keep.tile([P, N], U8, align_bytes=64)
        nc.gpsimd.memset(xs_raw[:].bitcast(I32), 0)
        nc.gpsimd.memset(w1s_raw[:].bitcast(I32), 0)
        ident = keep.tile([P, P], F32)
        make_identity(nc, ident[:])
        nc.vector.memset(xs_second[:].bitcast(I32), 0)
        nc.vector.memset(w2s[:].bitcast(I32), 0)

        offs_sb = keep.tile([P, S // 16], U16)
        nc.sync.dma_start(offs_sb[:], offs)
        for q in range(4):
            nc.sync.dma_start(
                out=xs_raw[32 * q : 32 * q + 8, :].bitcast(I32), in_=x_scales[:, 4 * q : 4 * q + 4, :].bitcast(I32)
            )
        xw_raw = [keep.tile([P, T], I32, name=f"xw_raw{o}", align_bytes=64) for o in range(PASSES)]
        nc.sync.dma_start(out=xw_raw[1][:], in_=x_words[1].rearrange("p n r -> p (n r)").bitcast(I32))
        for q in range(4):
            nc.sync.dma_start(
                out=w1s_raw[32 * q : 32 * q + 4, :].bitcast(I32).rearrange("r (o n) -> r o n", o=PASSES),
                in_=w1_scales[:, 4 * q : 4 * q + 4, :].bitcast(I32).rearrange("o r n -> r o n"),
            )
        w1w_raw = keep.tile([P, PASSES, 2 * H], U8, align_bytes=64)
        nc.sync.dma_start(out=w1w_raw[:].bitcast(I32), in_=w1_words.bitcast(I32).rearrange("o p n -> p o n"))
        nc.sync.dma_start(out=xw_raw[0][:], in_=x_words[0].rearrange("p n r -> p (n r)").bitcast(I32))
        thr_rows = thr.rearrange("(p t) j -> p t j", t=PACK)
        thr_sb = [keep.tile([P, S], F32, name=f"thr_sb{t}") for t in range(PACK)]
        cn3_sb = keep.tile([P, S // 16], U16)
        nc.sync.dma_start(cn3_sb[:], cn3)
        cn1_sb = keep.tile([P, S // 16], U16)
        nc.sync.dma_start(cn1_sb[:], cn1)
        cn2_sb = keep.tile([P, S // 16], U16)
        nc.sync.dma_start(cn2_sb[:], cn2)
        xs_both = keep.tile([P, S], U8, align_bytes=64)
        nc.vector.tensor_copy(xs_both[:], xs_raw[:].indirect(offs_sb[:]))
        for q in range(4):
            nc.sync.dma_start(
                out=xs_second[32 * q : 32 * q + 4, :].bitcast(I32), in_=xs_both[32 * q + 4 : 32 * q + 8, :].bitcast(I32)
            )
        for t in range(PACK):
            nc.sync.dma_start(out=thr_sb[t][:], in_=thr_rows[:, t, :])
        unit_sb = keep.tile([P, PACK], F32)
        nc.sync.dma_start(out=unit_sb[:], in_=unit.rearrange("(p t) o -> p (t o)", t=PACK))
        w2w = keep.tile([P, 2 * N], U8, align_bytes=64)
        nc.sync.dma_start(out=w2w[:].bitcast(I32), in_=w2_words[0].bitcast(I32))
        for q in range(4):
            nc.sync.dma_start(
                out=w2s[32 * q : 32 * q + 4, :].bitcast(I32), in_=w2_scales[0, 4 * q : 4 * q + 4, :].bitcast(I32)
            )

        ones = keep.tile([P, P], F32)
        nc.vector.memset(ones[:], 1.0)
        shift = keep.tile([P, P], F32)
        nc.vector.tensor_scalar(shift[:], ones[:], -SHIFT, 0.0, ALU.mult, ALU.add)
        tanh_bias = keep.tile([P, 1], F32)
        nc.vector.tensor_scalar(tanh_bias[:], ones[:, 0:1], -0.5 * math.log(2.5), 0.0, ALU.mult, ALU.add)
        row_scale = keep.tile([P, PACK], F32)
        nc.vector.tensor_scalar(row_scale[:], unit_sb[:], ROW, 0.0, ALU.mult, ALU.add)
        row_plain = keep.tile([P, PACK], F32)
        nc.vector.tensor_scalar(row_plain[:], unit_sb[:], ROW * 0.45, 0.0, ALU.mult, ALU.add)
        row_bias = keep.tile([P, PACK], F32)
        nc.vector.tensor_scalar(row_bias[:], unit_sb[:], ROW * SHIFT, 0.0, ALU.mult, ALU.add)

        def add_transposed(bank, src, start, stop):
            for b in range(S // P):
                cols = slice(b * P, (b + 1) * P)
                nc.tensor.matmul(
                    bank[:, cols],
                    lhsT=src(cols),
                    rhs=ident[:],
                    is_transpose=True,
                    start=start and b == 0,
                    stop=stop and b == S // P - 1,
                )

        gate_win = [keep.tile([P, 4 * S], F32, name=f"gate_win{t}") for t in range(PACK)]
        rate_win = [keep.tile([P, 2 * S], F32, name=f"rate_win{t}") for t in range(PACK)]
        drive = {}

        def deal(first, count, tag):
            dealt = keep.tile([P, count * PASSES * 3 * P], U8, name="dealt", tag=tag, align_bytes=64)
            words = dealt[:, : count * PASSES * 2 * P].rearrange("p (t o c) -> p t o c", t=count, o=PASSES)
            scales = dealt[:, count * PASSES * 2 * P :].rearrange("p (t o m) -> p t o m", t=count, o=PASSES)
            nc.vector.tensor_copy(
                words.rearrange("p t o (m b) -> p o t m b", b=2),
                w1w_raw[:].rearrange("p o (m t b) -> p o t m b", t=PACK, b=2)[:, :, first : first + count],
            )
            nc.vector.tensor_copy(
                scales.rearrange("p t o m -> p o t m"),
                w1s_raw[:].rearrange("p (o m t) -> p o t m", o=PASSES, t=PACK)[:, :, first : first + count],
            )
            return [(words[:, t], scales[:, t]) for t in range(count)]

        xw = [keep.tile([P, S], U32, name=f"xw{o}", align_bytes=64) for o in range(PASSES)]
        xs = [xs_both, xs_second]
        nc.vector.tensor_copy(xw[1][:], xw_raw[1][:].bitcast(U32).indirect(offs_sb[:]))
        w1 = deal(0, 1, "dealt_first")
        nc.vector.tensor_copy(xw[0][:], xw_raw[0][:].bitcast(U32).indirect(offs_sb[:]))
        w1 = w1 + deal(1, PACK - 1, "xw_raw0")

        closed = [keep.tile([P, S], F32, name=f"closed{t}") for t in range(PACK)]
        filled = [keep.tile([P, S], F32, name=f"filled{t}") for t in range(PACK)]
        hid = keep.tile([P, PACK, S], BF16, align_bytes=64)
        bound = {}
        shifted = {}

        def drive_stage(t):
            y = psum.tile([P, S], F32, name="y", tag=f"bank{t % 2}")
            for o in reversed(range(PASSES)):
                nc.tensor.matmul_mx(
                    y[:],
                    lhsT=w1[t][0][:, o, :].bitcast(FP4X4),
                    lhsT_scale=w1[t][1][:, o, :],
                    rhs=xw[o][:].bitcast(FP8X4),
                    rhs_scale=xs[o][:],
                    start=o == PASSES - 1,
                    stop=o == 0,
                )
            win = gate_win[t]
            nc.scalar.activation(win[:, :S], y[:], ACT.Tanh, scale=-0.5)
            plain = MODE[t] == "N"
            if plain:
                own = part4.tile([P, S], F32, name="partial")
                nc.vector.scalar_tensor_tensor(own[:], win[:, :S], 0.45, thr_sb[t][:], ALU.mult, ALU.add)
            else:
                drive[t] = psum.tile([P, S], F32, name=f"drive{t}")
                add_transposed(drive[t], lambda cols: thr_sb[t][:, cols], True, False)
                nc.vector.tensor_scalar(closed[t][:], win[:, :S], 0.45, 0.45, ALU.mult, ALU.add)
                add_transposed(drive[t], lambda cols: closed[t][:, cols], False, False)
            n3 = near.tile([P, S], F32, name="n3")
            nc.scalar.activation(n3[:], win[:].indirect(cn3_sb[:]), ACT.Copy, scale=0.075)
            n1 = near.tile([P, S], F32, name="n1")
            nc.vector.tensor_scalar(
                n1[:], win[:].indirect(cn1_sb[:]), 0.25, -0.925 if plain else -1.375, ALU.mult, ALU.add
            )
            n2 = near.tile([P, S], F32, name="n2")
            if N2[t] == "V":
                nc.vector.tensor_scalar(n2[:], win[:].indirect(cn2_sb[:]), 0.15, 0.0, ALU.mult, ALU.add)
            else:
                nc.scalar.activation(n2[:], win[:].indirect(cn2_sb[:]), ACT.Copy, scale=0.15)
            if plain:
                two = part4.tile([P, S], F32, name="partial")
                nc.vector.tensor_tensor(two[:], own[:], n3[:], ALU.add)
                nc.vector.tensor_tensor(own[:], two[:], n1[:], ALU.add)
                drive[t] = keep.tile([P, S], F32, name=f"drive_sb{t}")
                nc.vector.tensor_tensor(drive[t][:], own[:], n2[:], ALU.add)
            else:
                add_transposed(drive[t], lambda cols: n3[:, cols], False, False)
                add_transposed(drive[t], lambda cols: n1[:, cols], False, False)
                add_transposed(drive[t], lambda cols: n2[:, cols], False, True)

        def bound_stage(t):
            size = ring.tile([P, S], F32, name="size")
            nc.scalar.activation(size[:], drive[t][:], ACT.Abs)
            bound[t] = ring.tile([P, S], F32, name="bound")
            nc.scalar.activation(bound[t][:], size[:], ACT.Tanh, bias=tanh_bias[:], scale=0.5)

        def rate_stage(t):
            if MODE[t] == "N":
                nc.vector.scalar_tensor_tensor(rate_win[t][:, :S], bound[t][:], 1.0, drive[t][:], ALU.add, ALU.mult)
                return
            rate_t = ring.tile([P, S], F32, name="rate_t")
            nc.vector.scalar_tensor_tensor(rate_t[:], bound[t][:], 1.0, drive[t][:], ALU.add, ALU.mult)
            shifted[t] = psum.tile([P, S], F32, name="shifted", tag=f"shifted{t}")
            add_transposed(shifted[t], lambda cols: shift[:], True, False)
            add_transposed(shifted[t], lambda cols: rate_t[:, cols], False, True)

        def window_stage(t):
            if MODE[t] == "N":
                low = part4.tile([P, S], F32, name="partial")
                nc.vector.tensor_scalar(low[:], rate_win[t][:, :S], 0.0, -SHIFT, ALU.min, ALU.add)
                nc.vector.scalar_tensor_tensor(closed[t][:], gate_win[t][:, :S], 1.0, low[:], ALU.add, ALU.mult)
                nc.vector.tensor_scalar(
                    filled[t][:], closed[t][:], 0.48 / 0.45, row_plain[:, t : t + 1], ALU.add, ALU.mult
                )
                return
            nc.scalar.activation(
                rate_win[t][:, :S], shifted[t][:], ACT.Identity, bias=row_bias[:, t : t + 1], scale=row_scale[:, t : t + 1]
            )
            nc.vector.scalar_tensor_tensor(filled[t][:], shifted[t][:], -SHIFT, closed[t][:], ALU.min, ALU.mult)

        def hidden_stage(t):
            win = rate_win[t]
            if HC[t] == "X":
                for a in range(2):
                    cols = slice(a * HALF, (a + 1) * HALF)
                    part = ring.tile([P, HALF], F32, name="part")
                    picked = win[:].indirect(cn1_sb[:, a * HALF // 16 : (a + 1) * HALF // 16])
                    if a == 0:
                        nc.scalar.activation(part[:], picked, ACT.Copy)
                    else:
                        nc.vector.tensor_copy(part[:], picked)
                    nc.vector.scalar_tensor_tensor(hid[:, t, cols], filled[t][:, cols], 0.0 if MODE[t] == "N" else 0.48, part[:], ALU.add, ALU.mult)
            else:
                hc = ring.tile([P, S], F32, name="hc")
                if HC[t] == "S":
                    nc.scalar.activation(hc[:], win[:].indirect(cn1_sb[:]), ACT.Copy)
                else:
                    nc.vector.tensor_copy(hc[:], win[:].indirect(cn1_sb[:]))
                nc.vector.scalar_tensor_tensor(hid[:, t, :], filled[t][:], 0.0 if MODE[t] == "N" else 0.48, hc[:], ALU.add, ALU.mult)

        stages = {"A": drive_stage, "B": bound_stage, "R": rate_stage, "W": window_stage, "H": hidden_stage}
        for word in ORDER.split():
            stages[word[0]](int(word[1]))

        for a in range(2):
            cols = slice(a * HALF, (a + 1) * HALF)
            woven = ring.tile([P, HALF, PACK], BF16, name="woven", align_bytes=64)
            nc.vector.tensor_copy(
                woven[:].rearrange("p (c i) t -> p c t i", i=4),
                hid[:, :, cols].rearrange("p t (c i) -> p c t i", i=4),
            )
            codes = ring.tile([P, HALF], U32, name="codes", align_bytes=64)
            scales = ring.tile([P, HALF], U8, name="scales", align_bytes=64)
            nc.vector.quantize_mx(codes[:].bitcast(FP8X4), scales[:], woven[:].rearrange("p j t -> p (j t)"))
            for b in range(N // P):
                acc = psum.tile([P, HALF], F32, name="acc", tag=("bank0", "bank1", "drive1", "drive2")[2 * a + b])
                nc.tensor.matmul_mx(
                    acc[:],
                    lhsT=w2w[:, 2 * P * b : 2 * P * (b + 1)].bitcast(FP4X4),
                    lhsT_scale=w2s[:, P * b : P * (b + 1)],
                    rhs=codes[:].bitcast(FP8X4),
                    rhs_scale=scales[:],
                    start=True,
                    stop=True,
                )
                result = keep.tile([P, HALF], F32, name=f"result{a}{b}")
                if a == 1 and b == 1:
                    nc.vector.tensor_copy(result[:], acc[:])
                else:
                    nc.scalar.copy(result[:], acc[:])
                nc.sync.dma_start(out=out[b * P : (b + 1) * P, cols], in_=result[:])
